import numpy as np
import ml_dtypes


def mxq(x, axis, fmt="e4m3"):
    dtype, down = {"e4m3": (ml_dtypes.float8_e4m3fn, 7), "e5m2": (ml_dtypes.float8_e5m2, 14)}[fmt]
    v = np.moveaxis(np.asarray(x, np.float32).astype(ml_dtypes.bfloat16).astype(np.float64), axis, -1)
    blocks = v.reshape(v.shape[:-1] + (-1, 32))
    amax = np.abs(blocks).max(-1, keepdims=True)
    byte = np.maximum(np.where(amax > 0, np.frexp(amax)[1] - 1 + 127, 0) - down, 1)
    scale = np.exp2(byte - 127.0)
    codes = (blocks / scale).astype(np.float32).astype(dtype).astype(np.float64)
    return np.moveaxis((codes * scale).reshape(v.shape), -1, axis)


WIDE = False


def mx_kscale(k):
    if not WIDE:
        return np.ones(k)
    levels = np.array([10, -10, 5, -5, 0])
    if k % 512:
        return np.exp2(np.random.permutation(np.resize(levels, k // 32))).repeat(32)
    a = np.empty((k // 512, 16))
    for p in range(k // 512):
        a[p, :8] = np.random.permutation(np.resize(levels, 8))
        for g in range(8):
            far = levels[np.abs(levels - a[p, g]) >= 10]
            a[p, g + 8] = far[np.random.randint(len(far))]
    return np.exp2(a.ravel()).repeat(32)


def f64(x):
    return np.asarray(x).astype(np.float64)


def striped(idx):
    return np.tile(idx.reshape(-1, 16).T, (8, 1)).astype(np.uint16)


def unstriped(offs):
    return offs[:16].T.reshape(-1).astype(np.int64)


E2M1 = np.array([0.0, 0.5, 1.0, 1.5, 2.0, 3.0, 4.0, 6.0, -0.0, -0.5, -1.0, -1.5, -2.0, -3.0, -4.0, -6.0])


def pack_weight(w, fmt):
    k, n = w.shape
    w = f64(np.asarray(w, np.float32).astype(ml_dtypes.bfloat16)).reshape(k // 32, 32, n)
    amax = np.abs(w).max(1)
    if fmt == "e4m3":
        byte = np.frexp(amax)[1] - 1 + 127 - 7
    else:
        mant, ex = np.frexp(amax / 6.0)
        byte = np.where(mant > 0.5, ex, ex - 1) + 127
    byte = np.clip(np.where(amax > 0, byte, 1), 1, 254)
    scaled = (w * np.exp2(127.0 - byte)[:, None, :]).reshape(k, n).astype(np.float32)
    by_word = np.ascontiguousarray(scaled.reshape(k // 512, 128, 4, n).transpose(0, 1, 3, 2))
    if fmt == "e4m3":
        words = by_word.astype(ml_dtypes.float8_e4m3fn).view(np.uint8)
    else:
        c = by_word.astype(ml_dtypes.float4_e2m1fn).view(np.uint8) & 0xF
        words = (c[..., 0::2] | (c[..., 1::2] << 4)).reshape(k // 512, 128, 2 * n)
    return np.ascontiguousarray(words), np.ascontiguousarray(byte.astype(np.uint8).reshape(k // 512, 16, n))


def unpack_weight(words, scales, fmt):
    g, _, n = scales.shape
    words = np.ascontiguousarray(words).reshape(g, 128, n, -1)
    if fmt == "e4m3":
        vals = words.view(ml_dtypes.float8_e4m3fn).astype(np.float64)
    else:
        nib = np.empty((g, 128, n, 4), np.uint8)
        nib[..., 0::2] = words & 0xF
        nib[..., 1::2] = words >> 4
        vals = E2M1[nib]
    vals = vals * np.repeat(np.exp2(scales.astype(np.float64) - 127.0), 8, axis=1)[..., None]
    return vals.transpose(0, 1, 3, 2).reshape(g * 512, n)


def gelu(v):
    return 0.5 * v * (1.0 + np.tanh(np.sqrt(2.0 / np.pi) * (v + 0.044715 * v**3)))


def striped8(idx):
    return np.concatenate([v.reshape(-1, 16).T for v in idx]).astype(np.uint16)


def unstriped8(offs):
    return np.stack([offs[16 * g:16 * g + 16].T.reshape(-1) for g in range(8)]).astype(np.int64)


def heads(h, wgt, idx8):
    r = np.arange(h.shape[0])
    return wgt[r // 4 % 128] * h[r[:, None], idx8[r % 512 // 64]]


def bf(x):
    return np.asarray(x, np.float32).astype(ml_dtypes.bfloat16)


def planes(Y):
    n, m = Y.shape
    b = f64(bf(Y)).reshape(n // 32, 32, m)
    amax = np.abs(b).max(1)
    byte = np.clip(np.where(amax > 0, np.frexp(amax)[1] - 1 + 127 - 7, 1), 1, 254)
    codes = (b * np.exp2(127.0 - byte)[:, None, :]).reshape(n, m).astype(np.float32).astype(ml_dtypes.float8_e4m3fn).view(np.uint8)
    words = codes.reshape(n // 512, 128, 4, m).transpose(0, 1, 3, 2)
    return np.ascontiguousarray(words), np.ascontiguousarray(byte.astype(np.uint8).reshape(n // 512, 16, m))


K, T, S, T2, P, H, N = 1024, 2048, 512, 1024, 512, 1024, 1024

def setup_inputs():
    n = np.random.standard_normal
    s = mx_kscale(K)[:, None]
    u = mx_kscale(H)[:, None]
    tab_words, tab_scales = pack_weight(n((K, T)) * s, "e4m3")
    w1_words, w1_scales = pack_weight(0.75 * n((K, H)) / np.sqrt(K) / s, "e2m1")
    w2 = (0.4 * n((K, H)) / np.sqrt(K) / s).astype(np.float32)
    phase = np.random.uniform(-0.7, 0.7, H).astype(np.float32)
    gain = (np.random.uniform(0.4, 1.0, H) * u[:, 0]).astype(np.float32)
    page0 = (n((H, T2)) * u).astype(np.float32)
    wgs = np.exp(0.3 * n((128, S))).astype(np.float32)
    wgt = np.repeat(np.random.uniform(0.5, 2.0, (8, P)), 16, axis=0).astype(np.float32)
    shift = (n(H) * u[:, 0]).astype(np.float32)
    w3 = (n((H, N)) / np.sqrt(H) / u * np.exp(0.8 * n(N))[None, :]).astype(np.float32)
    offs = striped(np.random.permutation(T)[:S])
    offs2 = striped(np.random.permutation(T2)[:S])
    offs3 = striped8(np.stack([np.random.permutation(T2)[:P] for _ in range(8)]))
    return {"tab_words": tab_words, "tab_scales": tab_scales, "offs": offs, "offs2": offs2, "offs3": offs3,
            "w1_words": w1_words, "w1_scales": w1_scales, "w2": w2, "phase": phase, "gain": gain,
            "page0": page0, "wgs": wgs, "wgt": wgt, "shift": shift, "w3": w3}

def reference(tab_words, tab_scales, offs, offs2, offs3, w1_words, w1_scales, w2, phase, gain, page0, wgs, wgt, shift, w3):
    v = unpack_weight(tab_words, tab_scales, "e4m3")[:, unstriped(offs)]
    w1 = unpack_weight(w1_words, w1_scales, "e2m1")
    grow = np.exp(w1.T @ v)
    turn = np.cos((mxq(f64(w2), 0, "e4m3").T @ v) + f64(phase)[:, None])
    h = f64(gain)[:, None] * grow * turn
    page = f64(page0).copy()
    page[:, unstriped(offs2)] = np.tile(f64(wgs), (H // 128, 1)) * h
    x = heads(page, f64(wgt), unstriped8(offs3)) + f64(shift)[:, None]
    y = mxq(f64(w3), 0, "e4m3").T @ mxq(x, 0, "e4m3")
    words, scales = planes(y)
    return y, words, scales

@@ -1,0 +1,342 @@
+import math
+from contextlib import ExitStack
+
+import concourse.mybir as mybir
+
+K, T, S, T2, M, H, N = 1024, 2048, 512, 1024, 512, 1024, 1024
+FLOPS = 2 * K * H * S * 2 + 2 * H * N * M
+
+F32 = mybir.dt.float32
+BF16 = mybir.dt.bfloat16
+I32 = mybir.dt.int32
+U32 = mybir.dt.uint32
+U16 = mybir.dt.uint16
+U8 = mybir.dt.uint8
+FP8X4 = mybir.dt.float8_e4m3fn_x4
+FP4X4 = mybir.dt.float4_e2m1fn_x4
+ALU = mybir.AluOpType
+ACT = mybir.ActivationFunctionType
+
+P = 128
+PACK = 4
+KP = P * PACK
+SLICES = H // P
+CHUNKS = ((0, 256), (256, 128), (384, 128))
+TURNS_ON_VECTOR = 2
+TWO_PI = 2.0 * math.pi
+
+
+def tile_list_lane_gap_features_kernel(
+    tc, tab_words, tab_scales, offs, offs2, offs3, w1_words, w1_scales, w2, phase, gain,
+    page0, wgs, wgt, shift, w3, out_0, out_1, out_2,
+):
+    nc = tc.nc
+    with ExitStack() as ctx:
+        lists = ctx.enter_context(tc.tile_pool(name="lists", bufs=1))
+        keep = ctx.enter_context(tc.tile_pool(name="keep", bufs=1))
+        raws = ctx.enter_context(tc.tile_pool(name="raws", bufs=6))
+        ring = ctx.enter_context(tc.tile_pool(name="ring", bufs=2))
+        psum = ctx.enter_context(tc.psum_pool(name="psum", bufs=1))
+
+        idx1 = lists.tile([P, S // 16], U16, name="idx1")
+        idx2 = lists.tile([P, S // 16], U16, name="idx2")
+        idx3 = lists.tile([P, M // 16], U16, name="idx3")
+
+        tab_sc = keep.tile([P, 2 * T], U8, name="tab_sc", align_bytes=64)
+        w1_sc_raw = keep.tile([P, 2 * H], U8, name="w1_sc_raw", align_bytes=64)
+        nc.vector.memset(tab_sc[:].bitcast(I32), 0)
+        nc.gpsimd.memset(w1_sc_raw[:].bitcast(I32), 0)
+
+        nc.sync.dma_start(idx1[:], offs)
+        w1_raw = keep.tile([P, 2, H // 2], I32, name="w1_raw", align_bytes=64)
+        nc.sync.dma_start(w1_raw[:], w1_words.rearrange("a p n -> p a n").bitcast(I32))
+        for q in range(4):
+            nc.sync.dma_start(
+                tab_sc[32 * q:32 * q + 4, :].bitcast(I32).rearrange("r (a n) -> r a n", a=2),
+                tab_scales[:, 4 * q:4 * q + 4, :].rearrange("a r n -> r a n").bitcast(I32),
+            )
+        tab = []
+
+        def load_table(a):
+            tw = keep.tile([P, T], I32, name="tab%d" % a, tag="big%d" % a, align_bytes=64)
+            nc.sync.dma_start(tw[:], tab_words[a].rearrange("p t i -> p (t i)").bitcast(I32))
+            tab.append(tw)
+
+        load_table(0)
+        for q in range(4):
+            nc.sync.dma_start(
+                w1_sc_raw[32 * q:32 * q + 4, :].bitcast(I32).rearrange("r (a n) -> r a n", a=2),
+                w1_scales[:, 4 * q:4 * q + 4, :].rearrange("a r n -> r a n").bitcast(I32),
+            )
+        load_table(1)
+        vecs = {}
+
+        def load_vector(name, vec):
+            vt = keep.tile([P, 2, PACK], F32, name="vec_" + name)
+            nc.sync.dma_start(vt[:], vec.rearrange("(b p t) -> p b t", p=P, t=PACK))
+            vecs[name] = vt
+
+        def column(name, s):
+            return vecs[name][:, s // PACK, s % PACK:s % PACK + 1]
+
+        raw_w = {}
+
+        def load_weight(name, w, a, b):
+            raw = raws.tile([P, PACK, KP], F32, name="raw", tag="raw")
+            nc.sync.dma_start(
+                raw[:], w[KP * a:KP * (a + 1), KP * b:KP * (b + 1)].rearrange("(p j) c -> p j c", j=PACK))
+            raw_w[name, a, b] = raw
+
+        pages = {}
+
+        def load_page(s):
+            pg = keep.tile([P, T2], F32, name="page%d" % s)
+            nc.sync.dma_start(pg[:], page0.rearrange("(b p t) c -> b t p c", p=P, t=PACK)[s // PACK, s % PACK])
+            pages[s] = pg
+
+        wgs_t = keep.tile([P, PACK, S], F32, name="wgs_t", tag="swap1", align_bytes=64)
+
+        def load_wgs(pair):
+            rows = wgs.rearrange("(q t) j -> q t j", t=PACK)
+            for quad in (0, 2, 1, 3):
+                nc.sync.dma_start(wgs_t[32 * quad:32 * quad + 32, 2 * pair:2 * pair + 2, :],
+                                  rows[:, 2 * pair:2 * pair + 2, :])
+
+        wgt_t = keep.tile([P, M], F32, name="wgt_t")
+
+        load_weight("w2", w2, 0, 0)
+        load_vector("phase", phase)
+        load_weight("w2", w2, 1, 0)
+        load_vector("gain", gain)
+        nc.sync.dma_start(idx2[:], offs2)
+        load_page(0)
+        load_wgs(0)
+        nc.sync.dma_start(idx3[:], offs3)
+        nc.sync.dma_start(wgt_t[:], wgt)
+        load_vector("shift", shift)
+        load_weight("w2", w2, 0, 1)
+        load_page(1)
+        load_weight("w2", w2, 1, 1)
+        load_wgs(1)
+        load_page(2)
+        load_weight("w3", w3, 0, 0)
+        load_weight("w3", w3, 0, 1)
+        load_page(3)
+        load_weight("w3", w3, 1, 0)
+        load_page(4)
+        load_weight("w3", w3, 1, 1)
+        load_page(5)
+        load_page(6)
+        load_page(7)
+
+        w1_c = [keep.tile([P, 2, 2 * KP], U8, name="w1_c%d" % b, align_bytes=64) for b in range(2)]
+        w1_s = [keep.tile([P, 2, KP], U8, name="w1_s%d" % b, align_bytes=64) for b in range(2)]
+
+        def deal_words(b):
+            nc.vector.tensor_copy(
+                w1_c[b][:].bitcast(U16).rearrange("p a (t q) -> p a q t", t=PACK),
+                w1_raw[:].bitcast(U16)[:, :, KP * b:KP * (b + 1)].rearrange("p a (q t) -> p a q t", t=PACK),
+            )
+
+        def deal_scales(b):
+            nc.vector.tensor_copy(
+                w1_s[b][:].rearrange("p a (t q) -> p a q t", t=PACK),
+                w1_sc_raw[:].rearrange("p (a b q t) -> p b a q t", a=2, b=2, t=PACK)[:, b],
+            )
+
+        deal_words(0)
+
+        v_c, v_s = [], []
+        for a in range(2):
+            vs = keep.tile([P, S], U8, name="v_s%d" % a, align_bytes=64)
+            nc.vector.tensor_copy(vs[:], tab_sc[:, T * a:T * (a + 1)].indirect(idx1[:]))
+            v_s.append(vs)
+            vc = keep.tile([P, S], U32, name="v_c%d" % a, align_bytes=64)
+            nc.vector.tensor_copy(vc[:], tab[a][:].bitcast(U32).indirect(idx1[:]))
+            v_c.append(vc)
+            if a == 0:
+                deal_scales(0)
+        deal_words(1)
+        deal_scales(1)
+
+        def bank(i, shape):
+            return psum.tile(shape, F32, name="bank%d" % i, tag="bank%d" % i)
+
+        grow_acc = [bank(s, [P, S]) for s in range(SLICES)]
+        grow = []
+        for s in range(SLICES):
+            for a in range(2):
+                b, t = divmod(s, PACK)
+                nc.tensor.matmul_mx(
+                    out=grow_acc[s][:],
+                    lhsT=w1_c[b][:, a, 2 * P * t:2 * P * (t + 1)].bitcast(FP4X4),
+                    lhsT_scale=w1_s[b][:, a, P * t:P * (t + 1)],
+                    rhs=v_c[a][:].bitcast(FP8X4), rhs_scale=v_s[a][:],
+                    start=(a == 0), stop=(a == 1),
+                )
+                if a == 1:
+                    e = keep.tile([P, S], F32, name="grow%d" % s)
+                    nc.scalar.activation(e[:], grow_acc[s][:], ACT.Exp)
+                    grow.append(e)
+
+        codes, scales = {}, {}
+
+        rounded_w = {}
+
+        def round_weight(name, a, b, copy, stage):
+            rounded = keep.tile([P, PACK * KP], BF16, name="rounded", tag="stage%d" % stage, align_bytes=64)
+            copy(rounded[:].rearrange("p (t q j) -> p q j t", t=PACK, j=PACK),
+                 raw_w[name, a, b][:].rearrange("p j (q t) -> p q j t", t=PACK))
+            rounded_w[name, a, b] = rounded
+
+        def quantise_weight(name, a, b):
+            rounded = rounded_w[name, a, b]
+            c = keep.tile([P, KP], U32, name="%s_c%d%d" % (name, a, b), align_bytes=64)
+            sc = keep.tile([P, KP], U8, name="%s_s%d%d" % (name, a, b), align_bytes=64)
+            nc.vector.quantize_mx(out=c[:].bitcast(FP8X4), scales=sc[:], in_=rounded[:])
+            codes[name, a, b], scales[name, a, b] = c, sc
+
+        quarter = keep.tile([P, 2, PACK], F32, name="quarter")
+        nc.vector.tensor_scalar(quarter[:], vecs["phase"][:], 0.5 * math.pi, None, ALU.add)
+        vecs["quarter"] = quarter
+
+        counted, cosine, features = {}, {}, {}
+
+        def angle(s):
+            b, t = divmod(s, PACK)
+            acc = bank(s, [P, S])
+            for a in range(2):
+                nc.tensor.matmul_mx(
+                    out=acc[:],
+                    lhsT=codes["w2", a, b][:, P * t:P * (t + 1)].bitcast(FP8X4),
+                    lhsT_scale=scales["w2", a, b][:, P * t:P * (t + 1)],
+                    rhs=v_c[a][:].bitcast(FP8X4), rhs_scale=v_s[a][:],
+                    start=(a == 0), stop=(a == 1),
+                )
+            turns = ring.tile([P, S], I32, name="turns", tag="turns")
+            if s < TURNS_ON_VECTOR:
+                nc.vector.tensor_scalar(turns[:], acc[:], column("quarter", s), 1.0 / TWO_PI, ALU.add, ALU.mult)
+                counted[s] = (turns, acc, column("quarter", s))
+            else:
+                z = ring.tile([P, S], F32, name="size", tag="size")
+                nc.scalar.activation(z[:], acc[:], ACT.Abs, bias=column("phase", s))
+                nc.scalar.activation(turns[:].bitcast(U32), z[:], ACT.Copy, bias=0.25, scale=1.0 / TWO_PI)
+                counted[s] = (turns, z, 0.5 * math.pi)
+
+        def cosine_of(s):
+            turns, z, rest = counted[s]
+            r = keep.tile([P, S], F32, name="reduced", tag="stage%d" % (s % 2), align_bytes=64)
+            c = ring.tile([P, S], F32, name="cosine", tag="cosine")
+            nc.vector.scalar_tensor_tensor(r[:], turns[:], -TWO_PI, z[:], ALU.mult, ALU.add)
+            nc.scalar.activation(c[:], r[:], ACT.Sin, bias=rest)
+            cosine[s] = c
+
+        def feature(s):
+            h = ring.tile([P, S], F32, name="h", tag="h")
+            nc.vector.scalar_tensor_tensor(h[:], grow[s][:], column("gain", s), cosine[s][:], ALU.mult, ALU.mult)
+            features[s] = h
+
+        def put(s):
+            nc.vector.tensor_tensor(pages[s][:].indirect(idx2[:]), features[s][:], wgs_t[:, s % PACK, :], ALU.mult)
+
+        planes = {}
+
+        def pick(s, picked, m0, w):
+            nc.vector.tensor_tensor(
+                picked, pages[s][:].indirect(idx3[:, m0 // 16:(m0 + w) // 16]), wgt_t[:, m0:m0 + w], ALU.mult)
+            b, t = divmod(s, PACK)
+            if t == 0:
+                planes[b, m0] = ring.tile([P, PACK, w], BF16, name="planes", tag="planes")
+            nc.scalar.activation(planes[b, m0][:, t, :], picked, ACT.Identity, bias=column("shift", s))
+
+        def weave(copy, src, w, pool, tag):
+            woven = pool.tile([P, w, PACK], BF16, name="woven", tag=tag, align_bytes=64)
+            copy(woven[:].rearrange("p (c i) t -> p c t i", i=4), src.rearrange("p t (c i) -> p c t i", i=4))
+            return woven
+
+        accs = {}
+
+        def project(b, ci):
+            m0, w = CHUNKS[ci]
+            woven = weave(nc.scalar.copy, planes[b, m0][:], w, keep, "swap%d" % ((b + 1) % 2 if ci else 0))
+            xc = keep.tile([P, w], U32, name="x_c%d%d" % (b, ci), align_bytes=64)
+            xs = keep.tile([P, w], U8, name="x_s%d%d" % (b, ci), align_bytes=64)
+            nc.vector.quantize_mx(out=xc[:].bitcast(FP8X4), scales=xs[:], in_=woven[:].rearrange("p m t -> p (m t)"))
+            per_bank = 512 // w
+            for g in range(2):
+                for t in range(PACK):
+                    u = t // per_bank
+                    if b == 0 and t % per_bank == 0:
+                        accs[ci, g, u] = bank((m0 * SLICES) // M + g * (PACK // per_bank) + u, [P, per_bank, w])
+                    nc.tensor.matmul_mx(
+                        out=accs[ci, g, u][:, t % per_bank, :],
+                        lhsT=codes["w3", b, g][:, P * t:P * (t + 1)].bitcast(FP8X4),
+                        lhsT_scale=scales["w3", b, g][:, P * t:P * (t + 1)],
+                        rhs=xc[:].bitcast(FP8X4), rhs_scale=xs[:],
+                        start=(b == 0 and t % per_bank == 0),
+                        stop=(b == 1 and t % per_bank == per_bank - 1),
+                    )
+
+        y_c = keep.tile([P, 2, M], U32, name="y_c", align_bytes=64)
+        y_s = keep.tile([P, 2, M], U8, name="y_s", align_bytes=64)
+        y_t = {}
+        y_rows = out_0.rearrange("(g p t) m -> g p t m", p=P, t=PACK)
+
+        def hand_out(ci):
+            m0, w = CHUNKS[ci]
+            per_bank = 512 // w
+            for g in range(2):
+                if g not in y_t:
+                    y_t[g] = keep.tile([P, PACK * M], F32, name="y%d" % g, tag="big%d" % g, align_bytes=64)
+                y = y_t[g][:, PACK * m0:PACK * (m0 + w)].rearrange("p (t m) -> p t m", t=PACK)
+                for u in range(PACK // per_bank):
+                    nc.scalar.copy(y[:, u * per_bank:(u + 1) * per_bank, :], accs[ci, g, u][:])
+                nc.sync.dma_start(y_rows[g][:, :, m0:m0 + w], y)
+                woven = weave(nc.vector.tensor_copy, y, w, ring, "woven_y")
+                nc.vector.quantize_mx(out=y_c[:, g, m0:m0 + w].bitcast(FP8X4), scales=y_s[:, g, m0:m0 + w],
+                                      in_=woven[:].rearrange("p m t -> p (m t)"))
+                nc.sync.dma_start(
+                    out_1[g].rearrange("p m t -> p (m t)").bitcast(I32)[:, m0:m0 + w],
+                    y_c[:, g, m0:m0 + w].bitcast(I32))
+
+        for a in range(2):
+            round_weight("w2", a, 0, nc.vector.tensor_copy, a)
+            quantise_weight("w2", a, 0)
+        later = [("w2", 0, 1), ("w2", 1, 1), ("w3", 0, 0), ("w3", 0, 1), ("w3", 1, 0), ("w3", 1, 1)]
+        first_m0, first_w = CHUNKS[0]
+        early = keep.tile([P, SLICES, first_w], F32, name="early")
+        angle(0)
+        cosine_of(0)
+        angle(1)
+        cosine_of(1)
+        feature(0)
+        for s in range(SLICES):
+            put(s)
+            if s + 1 < SLICES:
+                feature(s + 1)
+            if s < len(later):
+                round_weight(*later[s], nc.scalar.copy, s % 2)
+                quantise_weight(*later[s])
+            if s + 2 < SLICES:
+                angle(s + 2)
+            pick(s, early[:, s, :], first_m0, first_w)
+            if s + 2 < SLICES:
+                cosine_of(s + 2)
+            if s % PACK == PACK - 1:
+                project(s // PACK, 0)
+
+        for ci in range(1, len(CHUNKS)):
+            m0, w = CHUNKS[ci]
+            for b in range(2):
+                late = keep.tile([P, PACK, w], F32, name="late", tag="swap%d" % ((b + 1) % 2), align_bytes=64)
+                for t in range(PACK):
+                    pick(PACK * b + t, late[:, t, :], m0, w)
+                project(b, ci)
+            hand_out(ci - 1)
+        hand_out(len(CHUNKS) - 1)
+
+        for q in range(4):
+            engine = nc.sync if q % 2 == 0 else nc.scalar
+            engine.dma_start(
+                out_2[:, 4 * q:4 * q + 4, :].rearrange("g r m -> r g m").bitcast(I32),
+                y_s[32 * q:32 * q + 4, :, :].bitcast(I32))

@@ -22,6 +22,9 @@ PACK = 4
 KP = P * PACK
 SLICES = H // P
 CHUNKS = ((0, 256), (256, 128), (384, 128))
+EARLY = 2
+Y_WEAVE = "vvv"
+Y_EVAC = ("ssss","ss","ss")
 TURNS_ON_VECTOR = 2
 TWO_PI = 2.0 * math.pi
 
@@ -48,13 +51,13 @@ def tile_list_lane_gap_features_kernel(
         nc.gpsimd.memset(w1_sc_raw[:].bitcast(I32), 0)
 
         nc.sync.dma_start(idx1[:], offs)
-        w1_raw = keep.tile([P, 2, H // 2], I32, name="w1_raw", align_bytes=64)
-        nc.sync.dma_start(w1_raw[:], w1_words.rearrange("a p n -> p a n").bitcast(I32))
         for q in range(4):
             nc.sync.dma_start(
-                tab_sc[32 * q:32 * q + 4, :].bitcast(I32).rearrange("r (a n) -> r a n", a=2),
-                tab_scales[:, 4 * q:4 * q + 4, :].rearrange("a r n -> r a n").bitcast(I32),
+                tab_sc[q:P:32, :].bitcast(I32).rearrange("r (a n) -> r a n", a=2),
+                tab_scales[:, q:16:4, :].rearrange("a r n -> r a n").bitcast(I32),
             )
+        w1_raw = keep.tile([P, 2, H // 2], I32, name="w1_raw", align_bytes=64)
+        nc.sync.dma_start(w1_raw[:], w1_words.rearrange("a p n -> p a n").bitcast(I32))
         tab = []
 
         def load_table(a):
@@ -65,8 +68,8 @@ def tile_list_lane_gap_features_kernel(
         load_table(0)
         for q in range(4):
             nc.sync.dma_start(
-                w1_sc_raw[32 * q:32 * q + 4, :].bitcast(I32).rearrange("r (a n) -> r a n", a=2),
-                w1_scales[:, 4 * q:4 * q + 4, :].rearrange("a r n -> r a n").bitcast(I32),
+                w1_sc_raw[q:P:32, :].bitcast(I32).rearrange("r (a n) -> r a n", a=2),
+                w1_scales[:, q:16:4, :].rearrange("a r n -> r a n").bitcast(I32),
             )
         load_table(1)
         vecs = {}
@@ -94,7 +97,7 @@ def tile_list_lane_gap_features_kernel(
             nc.sync.dma_start(pg[:], page0.rearrange("(b p t) c -> b t p c", p=P, t=PACK)[s // PACK, s % PACK])
             pages[s] = pg
 
-        wgs_t = keep.tile([P, PACK, S], F32, name="wgs_t", tag="swap1", align_bytes=64)
+        wgs_t = keep.tile([P, PACK, S], F32, name="wgs_t")
 
         def load_wgs(pair):
             rows = wgs.rearrange("(q t) j -> q t j", t=PACK)
@@ -105,8 +108,8 @@ def tile_list_lane_gap_features_kernel(
         wgt_t = keep.tile([P, M], F32, name="wgt_t")
 
         load_weight("w2", w2, 0, 0)
-        load_vector("phase", phase)
         load_weight("w2", w2, 1, 0)
+        load_vector("phase", phase)
         load_vector("gain", gain)
         nc.sync.dma_start(idx2[:], offs2)
         load_page(0)
@@ -114,8 +117,8 @@ def tile_list_lane_gap_features_kernel(
         nc.sync.dma_start(idx3[:], offs3)
         nc.sync.dma_start(wgt_t[:], wgt)
         load_vector("shift", shift)
-        load_weight("w2", w2, 0, 1)
         load_page(1)
+        load_weight("w2", w2, 0, 1)
         load_weight("w2", w2, 1, 1)
         load_wgs(1)
         load_page(2)
@@ -129,35 +132,36 @@ def tile_list_lane_gap_features_kernel(
         load_page(6)
         load_page(7)
 
-        w1_c = [keep.tile([P, 2, 2 * KP], U8, name="w1_c%d" % b, align_bytes=64) for b in range(2)]
-        w1_s = [keep.tile([P, 2, KP], U8, name="w1_s%d" % b, align_bytes=64) for b in range(2)]
+        w1_c, w1_s = {}, {}
 
-        def deal_words(b):
+        def deal_words(b, tag):
+            w1_c[b] = keep.tile([P, 2, 2 * KP], U8, name="w1_c%d" % b, tag=tag, align_bytes=64)
             nc.vector.tensor_copy(
                 w1_c[b][:].bitcast(U16).rearrange("p a (t q) -> p a q t", t=PACK),
                 w1_raw[:].bitcast(U16)[:, :, KP * b:KP * (b + 1)].rearrange("p a (q t) -> p a q t", t=PACK),
             )
 
-        def deal_scales(b):
+        def deal_scales(b, tag):
+            w1_s[b] = keep.tile([P, 2, KP], U8, name="w1_s%d" % b, tag=tag, align_bytes=64)
             nc.vector.tensor_copy(
                 w1_s[b][:].rearrange("p a (t q) -> p a q t", t=PACK),
                 w1_sc_raw[:].rearrange("p (a b q t) -> p b a q t", a=2, b=2, t=PACK)[:, b],
             )
-
-        deal_words(0)
 
         v_c, v_s = [], []
         for a in range(2):
             vs = keep.tile([P, S], U8, name="v_s%d" % a, align_bytes=64)
             nc.vector.tensor_copy(vs[:], tab_sc[:, T * a:T * (a + 1)].indirect(idx1[:]))
             v_s.append(vs)
+        deal_words(0, "w1_c0")
+        for a in range(2):
             vc = keep.tile([P, S], U32, name="v_c%d" % a, align_bytes=64)
             nc.vector.tensor_copy(vc[:], tab[a][:].bitcast(U32).indirect(idx1[:]))
             v_c.append(vc)
             if a == 0:
-                deal_scales(0)
-        deal_words(1)
-        deal_scales(1)
+                deal_scales(0, "w1_s0")
+        deal_words(1, "big1")
+        deal_scales(1, "big0")
 
         def bank(i, shape):
             return psum.tile(shape, F32, name="bank%d" % i, tag="bank%d" % i)
@@ -184,27 +188,29 @@ def tile_list_lane_gap_features_kernel(
         rounded_w = {}
 
         def round_weight(name, a, b, copy, stage):
-            rounded = keep.tile([P, PACK * KP], BF16, name="rounded", tag="stage%d" % stage, align_bytes=64)
+            rounded = keep.tile([P, PACK * KP], BF16, name="rounded", tag=stage, align_bytes=64)
             copy(rounded[:].rearrange("p (t q j) -> p q j t", t=PACK, j=PACK),
                  raw_w[name, a, b][:].rearrange("p j (q t) -> p q j t", t=PACK))
             rounded_w[name, a, b] = rounded
 
-        def quantise_weight(name, a, b):
+        def quantise_weight(name, a, b, cuts=(0, KP)):
             rounded = rounded_w[name, a, b]
             c = keep.tile([P, KP], U32, name="%s_c%d%d" % (name, a, b), align_bytes=64)
             sc = keep.tile([P, KP], U8, name="%s_s%d%d" % (name, a, b), align_bytes=64)
-            nc.vector.quantize_mx(out=c[:].bitcast(FP8X4), scales=sc[:], in_=rounded[:])
+            for lo, hi in zip(cuts[:-1], cuts[1:]):
+                nc.vector.quantize_mx(out=c[:, lo:hi].bitcast(FP8X4), scales=sc[:, lo:hi],
+                                      in_=rounded[:, PACK * lo:PACK * hi])
             codes[name, a, b], scales[name, a, b] = c, sc
 
         quarter = keep.tile([P, 2, PACK], F32, name="quarter")
         nc.vector.tensor_scalar(quarter[:], vecs["phase"][:], 0.5 * math.pi, None, ALU.add)
         vecs["quarter"] = quarter
 
-        counted, cosine, features = {}, {}, {}
+        cosine, features = {}, {}
 
-        def angle(s):
+        def angle_sum(s):
             b, t = divmod(s, PACK)
-            acc = bank(s, [P, S])
+            acc = bank((SLICES - s) % SLICES, [P, S])
             for a in range(2):
                 nc.tensor.matmul_mx(
                     out=acc[:],
@@ -213,41 +219,62 @@ def tile_list_lane_gap_features_kernel(
                     rhs=v_c[a][:].bitcast(FP8X4), rhs_scale=v_s[a][:],
                     start=(a == 0), stop=(a == 1),
                 )
-            turns = ring.tile([P, S], I32, name="turns", tag="turns")
-            if s < TURNS_ON_VECTOR:
-                nc.vector.tensor_scalar(turns[:], acc[:], column("quarter", s), 1.0 / TWO_PI, ALU.add, ALU.mult)
-                counted[s] = (turns, acc, column("quarter", s))
-            else:
-                z = ring.tile([P, S], F32, name="size", tag="size")
-                nc.scalar.activation(z[:], acc[:], ACT.Abs, bias=column("phase", s))
-                nc.scalar.activation(turns[:].bitcast(U32), z[:], ACT.Copy, bias=0.25, scale=1.0 / TWO_PI)
-                counted[s] = (turns, z, 0.5 * math.pi)
+            return acc
+
+        def cosine_alone(s, tag):
+            acc = angle_sum(s)
+            turns = keep.tile([P, S], I32, name="turns", tag=tag, align_bytes=64)
+            r = keep.tile([P, S], F32, name="angle%d" % s, align_bytes=64)
+            nc.vector.tensor_scalar(turns[:], acc[:], column("quarter", s), 1.0 / TWO_PI, ALU.add, ALU.mult)
+            nc.vector.scalar_tensor_tensor(r[:], turns[:], -TWO_PI, acc[:], ALU.mult, ALU.add)
+            nc.scalar.activation(r[:], r[:], ACT.Sin, bias=column("quarter", s))
+            cosine[s] = r[:]
+
+        counted = {}
+
+        def count_turns(group, tag, angle_tag):
+            r = keep.tile([P, len(group), S], F32, name="angles", tag=angle_tag, align_bytes=64)
+            for i, s in enumerate(group):
+                nc.scalar.activation(r[:, i, :], angle_sum(s)[:], ACT.Abs, bias=column("phase", s))
+            turns = keep.tile([P, len(group), S], I32, name="turns", tag=tag, align_bytes=64)
+            nc.scalar.activation(turns[:].bitcast(U32), r[:], ACT.Copy, bias=0.25, scale=1.0 / TWO_PI)
+            counted[group] = (turns, r)
+
+        def reduce_angles(group):
+            turns, r = counted[group]
+            nc.vector.scalar_tensor_tensor(r[:], turns[:], -TWO_PI, r[:], ALU.mult, ALU.add)
+            for i, s in enumerate(group):
+                cosine[s] = r[:, i, :]
 
         def cosine_of(s):
-            turns, z, rest = counted[s]
-            r = keep.tile([P, S], F32, name="reduced", tag="stage%d" % (s % 2), align_bytes=64)
-            c = ring.tile([P, S], F32, name="cosine", tag="cosine")
-            nc.vector.scalar_tensor_tensor(r[:], turns[:], -TWO_PI, z[:], ALU.mult, ALU.add)
-            nc.scalar.activation(c[:], r[:], ACT.Sin, bias=rest)
-            cosine[s] = c
+            nc.scalar.activation(cosine[s], cosine[s], ACT.Sin, bias=0.5 * math.pi)
 
-        def feature(s):
-            h = ring.tile([P, S], F32, name="h", tag="h")
-            nc.vector.scalar_tensor_tensor(h[:], grow[s][:], column("gain", s), cosine[s][:], ALU.mult, ALU.mult)
+        def feature(s, tag=None):
+            h = grow[s] if tag is None else keep.tile([P, S], F32, name="h", tag=tag, align_bytes=64)
+            nc.vector.scalar_tensor_tensor(
+                h[:], grow[s][:], column("gain", s), wgs_t[:, s % PACK, :], ALU.mult, ALU.mult)
             features[s] = h
 
         def put(s):
-            nc.vector.tensor_tensor(pages[s][:].indirect(idx2[:]), features[s][:], wgs_t[:, s % PACK, :], ALU.mult)
+            nc.vector.tensor_tensor(pages[s][:].indirect(idx2[:]), features[s][:], cosine[s], ALU.mult)
 
-        planes = {}
+        planes, waiting = {}, []
 
-        def pick(s, picked, m0, w):
+        def pick(s, picked, m0, w, chunks):
             nc.vector.tensor_tensor(
                 picked, pages[s][:].indirect(idx3[:, m0 // 16:(m0 + w) // 16]), wgt_t[:, m0:m0 + w], ALU.mult)
+            waiting.append((s, picked, m0, w))
+
+        def add_shifts():
+            for s, picked, m0, w in waiting:
+                add_shift(s, picked, m0, w)
+            waiting.clear()
+
+        def add_shift(s, picked, m0, w):
             b, t = divmod(s, PACK)
-            if t == 0:
-                planes[b, m0] = ring.tile([P, PACK, w], BF16, name="planes", tag="planes")
-            nc.scalar.activation(planes[b, m0][:, t, :], picked, ACT.Identity, bias=column("shift", s))
+            if b not in planes:
+                planes[b] = keep.tile([P, PACK, M], BF16, name="planes%d" % b, tag="angle%d" % b, align_bytes=64)
+            nc.scalar.activation(planes[b][:, t, m0:m0 + w], picked, ACT.Identity, bias=column("shift", s))
 
         def weave(copy, src, w, pool, tag):
             woven = pool.tile([P, w, PACK], BF16, name="woven", tag=tag, align_bytes=64)
@@ -258,7 +285,7 @@ def tile_list_lane_gap_features_kernel(
 
         def project(b, ci):
             m0, w = CHUNKS[ci]
-            woven = weave(nc.scalar.copy, planes[b, m0][:], w, keep, "swap%d" % ((b + 1) % 2 if ci else 0))
+            woven = weave(nc.scalar.copy, planes[b][:, :, m0:m0 + w], w, keep, "swap%d" % ((b + 1) % 2 if ci >= EARLY else 0 if ci == 0 else 2))
             xc = keep.tile([P, w], U32, name="x_c%d%d" % (b, ci), align_bytes=64)
             xs = keep.tile([P, w], U8, name="x_s%d%d" % (b, ci), align_bytes=64)
             nc.vector.quantize_mx(out=xc[:].bitcast(FP8X4), scales=xs[:], in_=woven[:].rearrange("p m t -> p (m t)"))
@@ -277,7 +304,6 @@ def tile_list_lane_gap_features_kernel(
                         stop=(b == 1 and t % per_bank == per_bank - 1),
                     )
 
-        y_c = keep.tile([P, 2, M], U32, name="y_c", align_bytes=64)
         y_s = keep.tile([P, 2, M], U8, name="y_s", align_bytes=64)
         y_t = {}
         y_rows = out_0.rearrange("(g p t) m -> g p t m", p=P, t=PACK)
@@ -285,55 +311,85 @@ def tile_list_lane_gap_features_kernel(
         def hand_out(ci):
             m0, w = CHUNKS[ci]
             per_bank = 512 // w
+            y_c = keep.tile([P, 2, w], U32, name="y_c%d" % ci, align_bytes=64)
             for g in range(2):
                 if g not in y_t:
                     y_t[g] = keep.tile([P, PACK * M], F32, name="y%d" % g, tag="big%d" % g, align_bytes=64)
                 y = y_t[g][:, PACK * m0:PACK * (m0 + w)].rearrange("p (t m) -> p t m", t=PACK)
                 for u in range(PACK // per_bank):
-                    nc.scalar.copy(y[:, u * per_bank:(u + 1) * per_bank, :], accs[ci, g, u][:])
+                    evac = nc.scalar.copy if Y_EVAC[ci][g * (PACK // per_bank) + u] == "s" else nc.vector.tensor_copy
+                    evac(y[:, u * per_bank:(u + 1) * per_bank, :], accs[ci, g, u][:])
                 nc.sync.dma_start(y_rows[g][:, :, m0:m0 + w], y)
-                woven = weave(nc.vector.tensor_copy, y, w, ring, "woven_y")
-                nc.vector.quantize_mx(out=y_c[:, g, m0:m0 + w].bitcast(FP8X4), scales=y_s[:, g, m0:m0 + w],
+                woven = weave(nc.scalar.copy if Y_WEAVE[ci] == "s" else nc.vector.tensor_copy, y, w, ring, "woven_y")
+                nc.vector.quantize_mx(out=y_c[:, g, :].bitcast(FP8X4), scales=y_s[:, g, m0:m0 + w],
                                       in_=woven[:].rearrange("p m t -> p (m t)"))
-                nc.sync.dma_start(
-                    out_1[g].rearrange("p m t -> p (m t)").bitcast(I32)[:, m0:m0 + w],
-                    y_c[:, g, m0:m0 + w].bitcast(I32))
+            nc.sync.dma_start(
+                out_1.rearrange("g p m t -> p g (m t)").bitcast(I32)[:, :, m0:m0 + w], y_c[:].bitcast(I32))
 
         for a in range(2):
-            round_weight("w2", a, 0, nc.vector.tensor_copy, a)
-            quantise_weight("w2", a, 0)
+            round_weight("w2", a, 0, nc.vector.tensor_copy, "stage%d" % a)
+            quantise_weight("w2", a, 0, (0, P, KP) if a == 1 else (0, KP))
         later = [("w2", 0, 1), ("w2", 1, 1), ("w3", 0, 0), ("w3", 0, 1), ("w3", 1, 0), ("w3", 1, 1)]
-        first_m0, first_w = CHUNKS[0]
-        early = keep.tile([P, SLICES, first_w], F32, name="early")
-        angle(0)
-        cosine_of(0)
-        angle(1)
-        cosine_of(1)
+        early_w = CHUNKS[EARLY - 1][0] + CHUNKS[EARLY - 1][1]
+        cosine_alone(0, "angles23")
+        cosine_alone(1, "angles23")
         feature(0)
+        feature(1)
+        count_turns((2, 3), "turns0", "angles23")
+
+        def next_weight(i):
+            round_weight(*later[i], nc.scalar.copy, "angle0" if i == 0 else "stage%d" % (i % 2))
+            quantise_weight(*later[i])
+
         for s in range(SLICES):
             put(s)
+            if s == 1:
+                reduce_angles((2, 3))
+                next_weight(0)
+                next_weight(1)
+                cosine_of(2)
+                add_shifts()
+            elif s == 2:
+                add_shifts()
+                count_turns((4, 5), "turns0", "angles45")
+                reduce_angles((4, 5))
+                cosine_of(3)
+                count_turns((6, 7), "turns1", "swap1")
+                reduce_angles((6, 7))
+            elif 3 <= s < SLICES - 1:
+                next_weight(s - 1)
+                cosine_of(s + 1)
+                add_shifts()
+                if s == PACK:
+                    for ci in range(EARLY):
+                        project(0, ci)
+            if 1 <= s < SLICES - 1:
+                feature(s + 1, "turns0" if s == 2 else None)
+            early = ring.tile([P, early_w], F32, name="early", tag="early", bufs=3)
             if s + 1 < SLICES:
-                feature(s + 1)
-            if s < len(later):
-                round_weight(*later[s], nc.scalar.copy, s % 2)
-                quantise_weight(*later[s])
-            if s + 2 < SLICES:
-                angle(s + 2)
-            pick(s, early[:, s, :], first_m0, first_w)
-            if s + 2 < SLICES:
-                cosine_of(s + 2)
-            if s % PACK == PACK - 1:
-                project(s // PACK, 0)
+                pick(s, early[:], 0, early_w, range(EARLY))
+            else:
+                for ci in range(EARLY):
+                    m0, w = CHUNKS[ci]
+                    pick(s, early[:, m0:m0 + w], m0, w, [ci])
+        add_shifts()
+        for ci in range(EARLY):
+            project(1, ci)
 
-        for ci in range(1, len(CHUNKS)):
+        handed = 0
+        for ci in range(EARLY, len(CHUNKS)):
             m0, w = CHUNKS[ci]
             for b in range(2):
                 late = keep.tile([P, PACK, w], F32, name="late", tag="swap%d" % ((b + 1) % 2), align_bytes=64)
                 for t in range(PACK):
-                    pick(PACK * b + t, late[:, t, :], m0, w)
+                    pick(PACK * b + t, late[:, t, :], m0, w, [ci])
+                add_shifts()
                 project(b, ci)
-            hand_out(ci - 1)
-        hand_out(len(CHUNKS) - 1)
+                if handed < ci:
+                    hand_out(handed)
+                    handed = handed + 1
+        for ci in range(handed, len(CHUNKS)):
+            hand_out(ci)
 
         for q in range(4):
             engine = nc.sync if q % 2 == 0 else nc.scalar

@@ -179,7 +179,7 @@ def tile_list_lane_gap_features_kernel(
                     start=(a == 0), stop=(a == 1),
                 )
                 if a == 1:
-                    e = keep.tile([P, S], F32, name="grow%d" % s)
+                    e = keep.tile([P, S], F32, name="grow%d" % s, align_bytes=64)
                     nc.scalar.activation(e[:], grow_acc[s][:], ACT.Exp)
                     grow.append(e)
 
@@ -283,10 +283,22 @@ def tile_list_lane_gap_features_kernel(
 
         accs = {}
 
+        woven_x = {}
+
+        def weave_x(b, ci):
+            m0, w = CHUNKS[ci]
+            tag = "swap%d" % ((b + 1) % 2 if ci >= EARLY else 0 if ci == 0 else 2)
+            if b == 0 and ci < EARLY:
+                tag = "woven_x%d" % ci
+            woven_x[b, ci] = weave(nc.scalar.copy, planes[b][:, :, m0:m0 + w], w, keep, tag)
+
         def project(b, ci):
             m0, w = CHUNKS[ci]
-            woven = weave(nc.scalar.copy, planes[b][:, :, m0:m0 + w], w, keep, "swap%d" % ((b + 1) % 2 if ci >= EARLY else 0 if ci == 0 else 2))
-            xc = keep.tile([P, w], U32, name="x_c%d%d" % (b, ci), align_bytes=64)
+            if (b, ci) not in woven_x:
+                weave_x(b, ci)
+            woven = woven_x[b, ci]
+            xc = keep.tile([P, w], U32, name="x_c%d%d" % (b, ci), align_bytes=64,
+                           tag="grow7" if (b, ci) == (0, 0) else "x_c%d%d" % (b, ci))
             xs = keep.tile([P, w], U8, name="x_s%d%d" % (b, ci), align_bytes=64)
             nc.vector.quantize_mx(out=xc[:].bitcast(FP8X4), scales=xs[:], in_=woven[:].rearrange("p m t -> p (m t)"))
             per_bank = 512 // w
@@ -362,7 +374,7 @@ def tile_list_lane_gap_features_kernel(
                 add_shifts()
                 if s == PACK:
                     for ci in range(EARLY):
-                        project(0, ci)
+                        weave_x(0, ci)
             if 1 <= s < SLICES - 1:
                 feature(s + 1, "turns0" if s == 2 else None)
             early = ring.tile([P, early_w], F32, name="early", tag="early", bufs=3)
@@ -373,17 +385,23 @@ def tile_list_lane_gap_features_kernel(
                     m0, w = CHUNKS[ci]
                     pick(s, early[:, m0:m0 + w], m0, w, [ci])
         add_shifts()
-        for ci in range(EARLY):
-            project(1, ci)
+        for b in range(2):
+            for ci in range(EARLY):
+                project(b, ci)
 
         handed = 0
         for ci in range(EARLY, len(CHUNKS)):
             m0, w = CHUNKS[ci]
             for b in range(2):
-                late = keep.tile([P, PACK, w], F32, name="late", tag="swap%d" % ((b + 1) % 2), align_bytes=64)
+                late = keep.tile([P, PACK, w], F32, name="late", tag="swap%d" % (b + 1), align_bytes=64)
                 for t in range(PACK):
                     pick(PACK * b + t, late[:, t, :], m0, w, [ci])
-                add_shifts()
+                waiting.clear()
+                woven = keep.tile([P, w, PACK], BF16, name="woven_late", tag="swap0", align_bytes=64)
+                nc.vector.tensor_tensor(
+                    woven[:].rearrange("p (c i) t -> p c t i", i=4), late[:].rearrange("p t (c i) -> p c t i", i=4),
+                    vecs["shift"][:, b, :].unsqueeze(1).unsqueeze(3).to_broadcast([P, w // 4, PACK, 4]), ALU.add)
+                woven_x[b, ci] = woven
                 project(b, ci)
                 if handed < ci:
                     hand_out(handed)

import math
from contextlib import ExitStack

import concourse.mybir as mybir

K, T, S, T2, M, H, N = 1024, 2048, 512, 1024, 512, 1024, 1024
FLOPS = 2 * K * H * S * 2 + 2 * H * N * M

F32 = mybir.dt.float32
BF16 = mybir.dt.bfloat16
I32 = mybir.dt.int32
U32 = mybir.dt.uint32
U16 = mybir.dt.uint16
U8 = mybir.dt.uint8
FP8X4 = mybir.dt.float8_e4m3fn_x4
FP4X4 = mybir.dt.float4_e2m1fn_x4
ALU = mybir.AluOpType
ACT = mybir.ActivationFunctionType

P = 128
PACK = 4
KP = P * PACK
SLICES = H // P
CHUNKS = ((0, 256), (256, 128), (384, 128))
EARLY = 2
Y_WEAVE = "vvv"
Y_EVAC = ("ssss","ss","ss")
TURNS_ON_VECTOR = 2
TWO_PI = 2.0 * math.pi


def tile_list_lane_gap_features_kernel(
    tc, tab_words, tab_scales, offs, offs2, offs3, w1_words, w1_scales, w2, phase, gain,
    page0, wgs, wgt, shift, w3, out_0, out_1, out_2,
):
    nc = tc.nc
    with ExitStack() as ctx:
        lists = ctx.enter_context(tc.tile_pool(name="lists", bufs=1))
        keep = ctx.enter_context(tc.tile_pool(name="keep", bufs=1))
        raws = ctx.enter_context(tc.tile_pool(name="raws", bufs=6))
        ring = ctx.enter_context(tc.tile_pool(name="ring", bufs=2))
        psum = ctx.enter_context(tc.psum_pool(name="psum", bufs=1))

        idx1 = lists.tile([P, S // 16], U16, name="idx1")
        idx2 = lists.tile([P, S // 16], U16, name="idx2")
        idx3 = lists.tile([P, M // 16], U16, name="idx3")

        tab_sc = keep.tile([P, 2 * T], U8, name="tab_sc", align_bytes=64)
        w1_sc_raw = keep.tile([P, 2 * H], U8, name="w1_sc_raw", align_bytes=64)
        nc.vector.memset(tab_sc[:].bitcast(I32), 0)
        nc.gpsimd.memset(w1_sc_raw[:].bitcast(I32), 0)

        nc.sync.dma_start(idx1[:], offs)
        for q in range(4):
            nc.sync.dma_start(
                tab_sc[q:P:32, :].bitcast(I32).rearrange("r (a n) -> r a n", a=2),
                tab_scales[:, q:16:4, :].rearrange("a r n -> r a n").bitcast(I32),
            )
        w1_raw = keep.tile([P, 2, H // 2], I32, name="w1_raw", align_bytes=64)
        nc.sync.dma_start(w1_raw[:], w1_words.rearrange("a p n -> p a n").bitcast(I32))
        tab = []

        def load_table(a):
            tw = keep.tile([P, T], I32, name="tab%d" % a, tag="big%d" % a, align_bytes=64)
            nc.sync.dma_start(tw[:], tab_words[a].rearrange("p t i -> p (t i)").bitcast(I32))
            tab.append(tw)

        load_table(0)
        for q in range(4):
            nc.sync.dma_start(
                w1_sc_raw[q:P:32, :].bitcast(I32).rearrange("r (a n) -> r a n", a=2),
                w1_scales[:, q:16:4, :].rearrange("a r n -> r a n").bitcast(I32),
            )
        load_table(1)
        vecs = {}

        def load_vector(name, vec):
            vt = keep.tile([P, 2, PACK], F32, name="vec_" + name)
            nc.sync.dma_start(vt[:], vec.rearrange("(b p t) -> p b t", p=P, t=PACK))
            vecs[name] = vt

        def column(name, s):
            return vecs[name][:, s // PACK, s % PACK:s % PACK + 1]

        raw_w = {}

        def load_weight(name, w, a, b):
            raw = raws.tile([P, PACK, KP], F32, name="raw", tag="raw")
            nc.sync.dma_start(
                raw[:], w[KP * a:KP * (a + 1), KP * b:KP * (b + 1)].rearrange("(p j) c -> p j c", j=PACK))
            raw_w[name, a, b] = raw

        pages = {}

        def load_page(s):
            pg = keep.tile([P, T2], F32, name="page%d" % s)
            nc.sync.dma_start(pg[:], page0.rearrange("(b p t) c -> b t p c", p=P, t=PACK)[s // PACK, s % PACK])
            pages[s] = pg

        wgs_t = keep.tile([P, PACK, S], F32, name="wgs_t")

        def load_wgs(pair):
            rows = wgs.rearrange("(q t) j -> q t j", t=PACK)
            for quad in (0, 2, 1, 3):
                nc.sync.dma_start(wgs_t[32 * quad:32 * quad + 32, 2 * pair:2 * pair + 2, :],
                                  rows[:, 2 * pair:2 * pair + 2, :])

        wgt_t = keep.tile([P, M], F32, name="wgt_t")

        load_weight("w2", w2, 0, 0)
        load_weight("w2", w2, 1, 0)
        load_vector("phase", phase)
        load_vector("gain", gain)
        nc.sync.dma_start(idx2[:], offs2)
        load_page(0)
        load_wgs(0)
        nc.sync.dma_start(idx3[:], offs3)
        nc.sync.dma_start(wgt_t[:], wgt)
        load_vector("shift", shift)
        load_page(1)
        load_weight("w2", w2, 0, 1)
        load_weight("w2", w2, 1, 1)
        load_wgs(1)
        load_page(2)
        load_weight("w3", w3, 0, 0)
        load_weight("w3", w3, 0, 1)
        load_page(3)
        load_weight("w3", w3, 1, 0)
        load_page(4)
        load_weight("w3", w3, 1, 1)
        load_page(5)
        load_page(6)
        load_page(7)

        w1_c, w1_s = {}, {}

        def deal_words(b, tag):
            w1_c[b] = keep.tile([P, 2, 2 * KP], U8, name="w1_c%d" % b, tag=tag, align_bytes=64)
            nc.vector.tensor_copy(
                w1_c[b][:].bitcast(U16).rearrange("p a (t q) -> p a q t", t=PACK),
                w1_raw[:].bitcast(U16)[:, :, KP * b:KP * (b + 1)].rearrange("p a (q t) -> p a q t", t=PACK),
            )

        def deal_scales(b, tag):
            w1_s[b] = keep.tile([P, 2, KP], U8, name="w1_s%d" % b, tag=tag, align_bytes=64)
            nc.vector.tensor_copy(
                w1_s[b][:].rearrange("p a (t q) -> p a q t", t=PACK),
                w1_sc_raw[:].rearrange("p (a b q t) -> p b a q t", a=2, b=2, t=PACK)[:, b],
            )

        v_c, v_s = [], []
        for a in range(2):
            vs = keep.tile([P, S], U8, name="v_s%d" % a, align_bytes=64)
            nc.vector.tensor_copy(vs[:], tab_sc[:, T * a:T * (a + 1)].indirect(idx1[:]))
            v_s.append(vs)
        deal_words(0, "w1_c0")
        for a in range(2):
            vc = keep.tile([P, S], U32, name="v_c%d" % a, align_bytes=64)
            nc.vector.tensor_copy(vc[:], tab[a][:].bitcast(U32).indirect(idx1[:]))
            v_c.append(vc)
            if a == 0:
                deal_scales(0, "w1_s0")
        deal_words(1, "big1")
        deal_scales(1, "big0")

        def bank(i, shape):
            return psum.tile(shape, F32, name="bank%d" % i, tag="bank%d" % i)

        grow_acc = [bank(s, [P, S]) for s in range(SLICES)]
        grow = []
        for s in range(SLICES):
            for a in range(2):
                b, t = divmod(s, PACK)
                nc.tensor.matmul_mx(
                    out=grow_acc[s][:],
                    lhsT=w1_c[b][:, a, 2 * P * t:2 * P * (t + 1)].bitcast(FP4X4),
                    lhsT_scale=w1_s[b][:, a, P * t:P * (t + 1)],
                    rhs=v_c[a][:].bitcast(FP8X4), rhs_scale=v_s[a][:],
                    start=(a == 0), stop=(a == 1),
                )
                if a == 1:
                    e = keep.tile([P, S], F32, name="grow%d" % s, align_bytes=64)
                    nc.scalar.activation(e[:], grow_acc[s][:], ACT.Exp)
                    grow.append(e)

        codes, scales = {}, {}

        rounded_w = {}

        def round_weight(name, a, b, copy, stage):
            rounded = keep.tile([P, PACK * KP], BF16, name="rounded", tag=stage, align_bytes=64)
            copy(rounded[:].rearrange("p (t q j) -> p q j t", t=PACK, j=PACK),
                 raw_w[name, a, b][:].rearrange("p j (q t) -> p q j t", t=PACK))
            rounded_w[name, a, b] = rounded

        def quantise_weight(name, a, b, cuts=(0, KP)):
            rounded = rounded_w[name, a, b]
            c = keep.tile([P, KP], U32, name="%s_c%d%d" % (name, a, b), align_bytes=64)
            sc = keep.tile([P, KP], U8, name="%s_s%d%d" % (name, a, b), align_bytes=64)
            for lo, hi in zip(cuts[:-1], cuts[1:]):
                nc.vector.quantize_mx(out=c[:, lo:hi].bitcast(FP8X4), scales=sc[:, lo:hi],
                                      in_=rounded[:, PACK * lo:PACK * hi])
            codes[name, a, b], scales[name, a, b] = c, sc

        quarter = keep.tile([P, 2, PACK], F32, name="quarter")
        nc.vector.tensor_scalar(quarter[:], vecs["phase"][:], 0.5 * math.pi, None, ALU.add)
        vecs["quarter"] = quarter

        cosine, features = {}, {}

        def angle_sum(s):
            b, t = divmod(s, PACK)
            acc = bank((SLICES - s) % SLICES, [P, S])
            for a in range(2):
                nc.tensor.matmul_mx(
                    out=acc[:],
                    lhsT=codes["w2", a, b][:, P * t:P * (t + 1)].bitcast(FP8X4),
                    lhsT_scale=scales["w2", a, b][:, P * t:P * (t + 1)],
                    rhs=v_c[a][:].bitcast(FP8X4), rhs_scale=v_s[a][:],
                    start=(a == 0), stop=(a == 1),
                )
            return acc

        def cosine_alone(s, tag):
            acc = angle_sum(s)
            turns = keep.tile([P, S], I32, name="turns", tag=tag, align_bytes=64)
            r = keep.tile([P, S], F32, name="angle%d" % s, align_bytes=64)
            nc.vector.tensor_scalar(turns[:], acc[:], column("quarter", s), 1.0 / TWO_PI, ALU.add, ALU.mult)
            nc.vector.scalar_tensor_tensor(r[:], turns[:], -TWO_PI, acc[:], ALU.mult, ALU.add)
            nc.scalar.activation(r[:], r[:], ACT.Sin, bias=column("quarter", s))
            cosine[s] = r[:]

        counted = {}

        def count_turns(group, tag, angle_tag):
            r = keep.tile([P, len(group), S], F32, name="angles", tag=angle_tag, align_bytes=64)
            for i, s in enumerate(group):
                nc.scalar.activation(r[:, i, :], angle_sum(s)[:], ACT.Abs, bias=column("phase", s))
            turns = keep.tile([P, len(group), S], I32, name="turns", tag=tag, align_bytes=64)
            nc.scalar.activation(turns[:].bitcast(U32), r[:], ACT.Copy, bias=0.25, scale=1.0 / TWO_PI)
            counted[group] = (turns, r)

        def reduce_angles(group):
            turns, r = counted[group]
            nc.vector.scalar_tensor_tensor(r[:], turns[:], -TWO_PI, r[:], ALU.mult, ALU.add)
            for i, s in enumerate(group):
                cosine[s] = r[:, i, :]

        def cosine_of(s):
            nc.scalar.activation(cosine[s], cosine[s], ACT.Sin, bias=0.5 * math.pi)

        def feature(s, tag=None):
            h = grow[s] if tag is None else keep.tile([P, S], F32, name="h", tag=tag, align_bytes=64)
            nc.vector.scalar_tensor_tensor(
                h[:], grow[s][:], column("gain", s), wgs_t[:, s % PACK, :], ALU.mult, ALU.mult)
            features[s] = h

        def put(s):
            nc.vector.tensor_tensor(pages[s][:].indirect(idx2[:]), features[s][:], cosine[s], ALU.mult)

        planes, waiting = {}, []

        def pick(s, picked, m0, w, chunks):
            nc.vector.tensor_tensor(
                picked, pages[s][:].indirect(idx3[:, m0 // 16:(m0 + w) // 16]), wgt_t[:, m0:m0 + w], ALU.mult)
            waiting.append((s, picked, m0, w))

        def add_shifts():
            for s, picked, m0, w in waiting:
                add_shift(s, picked, m0, w)
            waiting.clear()

        def add_shift(s, picked, m0, w):
            b, t = divmod(s, PACK)
            if b not in planes:
                planes[b] = keep.tile([P, PACK, M], BF16, name="planes%d" % b, tag="angle%d" % b, align_bytes=64)
            nc.scalar.activation(planes[b][:, t, m0:m0 + w], picked, ACT.Identity, bias=column("shift", s))

        def weave(copy, src, w, pool, tag):
            woven = pool.tile([P, w, PACK], BF16, name="woven", tag=tag, align_bytes=64)
            copy(woven[:].rearrange("p (c i) t -> p c t i", i=4), src.rearrange("p t (c i) -> p c t i", i=4))
            return woven

        accs = {}

        woven_x = {}

        def weave_x(b, ci):
            m0, w = CHUNKS[ci]
            tag = "swap%d" % ((b + 1) % 2 if ci >= EARLY else 0 if ci == 0 else 2)
            if b == 0 and ci < EARLY:
                tag = "woven_x%d" % ci
            woven_x[b, ci] = weave(nc.scalar.copy, planes[b][:, :, m0:m0 + w], w, keep, tag)

        def project(b, ci):
            m0, w = CHUNKS[ci]
            if (b, ci) not in woven_x:
                weave_x(b, ci)
            woven = woven_x[b, ci]
            xc = keep.tile([P, w], U32, name="x_c%d%d" % (b, ci), align_bytes=64,
                           tag="grow7" if (b, ci) == (0, 0) else "x_c%d%d" % (b, ci))
            xs = keep.tile([P, w], U8, name="x_s%d%d" % (b, ci), align_bytes=64)
            nc.vector.quantize_mx(out=xc[:].bitcast(FP8X4), scales=xs[:], in_=woven[:].rearrange("p m t -> p (m t)"))
            per_bank = 512 // w
            for g in range(2):
                for t in range(PACK):
                    u = t // per_bank
                    if b == 0 and t % per_bank == 0:
                        accs[ci, g, u] = bank((m0 * SLICES) // M + g * (PACK // per_bank) + u, [P, per_bank, w])
                    nc.tensor.matmul_mx(
                        out=accs[ci, g, u][:, t % per_bank, :],
                        lhsT=codes["w3", b, g][:, P * t:P * (t + 1)].bitcast(FP8X4),
                        lhsT_scale=scales["w3", b, g][:, P * t:P * (t + 1)],
                        rhs=xc[:].bitcast(FP8X4), rhs_scale=xs[:],
                        start=(b == 0 and t % per_bank == 0),
                        stop=(b == 1 and t % per_bank == per_bank - 1),
                    )

        y_s = keep.tile([P, 2, M], U8, name="y_s", align_bytes=64)
        y_t = {}
        y_rows = out_0.rearrange("(g p t) m -> g p t m", p=P, t=PACK)

        def hand_out(ci):
            m0, w = CHUNKS[ci]
            per_bank = 512 // w
            y_c = keep.tile([P, 2, w], U32, name="y_c%d" % ci, align_bytes=64)
            for g in range(2):
                if g not in y_t:
                    y_t[g] = keep.tile([P, PACK * M], F32, name="y%d" % g, tag="big%d" % g, align_bytes=64)
                y = y_t[g][:, PACK * m0:PACK * (m0 + w)].rearrange("p (t m) -> p t m", t=PACK)
                for u in range(PACK // per_bank):
                    evac = nc.scalar.copy if Y_EVAC[ci][g * (PACK // per_bank) + u] == "s" else nc.vector.tensor_copy
                    evac(y[:, u * per_bank:(u + 1) * per_bank, :], accs[ci, g, u][:])
                nc.sync.dma_start(y_rows[g][:, :, m0:m0 + w], y)
                woven = weave(nc.scalar.copy if Y_WEAVE[ci] == "s" else nc.vector.tensor_copy, y, w, ring, "woven_y")
                nc.vector.quantize_mx(out=y_c[:, g, :].bitcast(FP8X4), scales=y_s[:, g, m0:m0 + w],
                                      in_=woven[:].rearrange("p m t -> p (m t)"))
            nc.sync.dma_start(
                out_1.rearrange("g p m t -> p g (m t)").bitcast(I32)[:, :, m0:m0 + w], y_c[:].bitcast(I32))

        for a in range(2):
            round_weight("w2", a, 0, nc.vector.tensor_copy, "stage%d" % a)
            quantise_weight("w2", a, 0, (0, P, KP) if a == 1 else (0, KP))
        later = [("w2", 0, 1), ("w2", 1, 1), ("w3", 0, 0), ("w3", 0, 1), ("w3", 1, 0), ("w3", 1, 1)]
        early_w = CHUNKS[EARLY - 1][0] + CHUNKS[EARLY - 1][1]
        cosine_alone(0, "angles23")
        cosine_alone(1, "angles23")
        feature(0)
        feature(1)
        count_turns((2, 3), "turns0", "angles23")

        def next_weight(i):
            round_weight(*later[i], nc.scalar.copy, "angle0" if i == 0 else "stage%d" % (i % 2))
            quantise_weight(*later[i])

        for s in range(SLICES):
            put(s)
            if s == 1:
                reduce_angles((2, 3))
                next_weight(0)
                next_weight(1)
                cosine_of(2)
                add_shifts()
            elif s == 2:
                add_shifts()
                count_turns((4, 5), "turns0", "angles45")
                reduce_angles((4, 5))
                cosine_of(3)
                count_turns((6, 7), "turns1", "swap1")
                reduce_angles((6, 7))
            elif 3 <= s < SLICES - 1:
                next_weight(s - 1)
                cosine_of(s + 1)
                add_shifts()
                if s == PACK:
                    for ci in range(EARLY):
                        weave_x(0, ci)
            if 1 <= s < SLICES - 1:
                feature(s + 1, "turns0" if s == 2 else None)
            early = ring.tile([P, early_w], F32, name="early", tag="early", bufs=3)
            if s + 1 < SLICES:
                pick(s, early[:], 0, early_w, range(EARLY))
            else:
                for ci in range(EARLY):
                    m0, w = CHUNKS[ci]
                    pick(s, early[:, m0:m0 + w], m0, w, [ci])
        add_shifts()
        for b in range(2):
            for ci in range(EARLY):
                project(b, ci)

        handed = 0
        for ci in range(EARLY, len(CHUNKS)):
            m0, w = CHUNKS[ci]
            for b in range(2):
                late = keep.tile([P, PACK, w], F32, name="late", tag="swap%d" % (b + 1), align_bytes=64)
                for t in range(PACK):
                    pick(PACK * b + t, late[:, t, :], m0, w, [ci])
                waiting.clear()
                woven = keep.tile([P, w, PACK], BF16, name="woven_late", tag="swap0", align_bytes=64)
                nc.vector.tensor_tensor(
                    woven[:].rearrange("p (c i) t -> p c t i", i=4), late[:].rearrange("p t (c i) -> p c t i", i=4),
                    vecs["shift"][:, b, :].unsqueeze(1).unsqueeze(3).to_broadcast([P, w // 4, PACK, 4]), ALU.add)
                woven_x[b, ci] = woven
                project(b, ci)
                if handed < ci:
                    hand_out(handed)
                    handed = handed + 1
        for ci in range(handed, len(CHUNKS)):
            hand_out(ci)

        for q in range(4):
            engine = nc.sync if q % 2 == 0 else nc.scalar
            engine.dma_start(
                out_2[:, 4 * q:4 * q + 4, :].rearrange("g r m -> r g m").bitcast(I32),
                y_s[32 * q:32 * q + 4, :, :].bitcast(I32))
